import numpy as np
import ml_dtypes


def mxq(x, axis, fmt="e4m3"):
    dtype, down = {"e4m3": (ml_dtypes.float8_e4m3fn, 7), "e5m2": (ml_dtypes.float8_e5m2, 14)}[fmt]
    v = np.moveaxis(np.asarray(x, np.float32).astype(ml_dtypes.bfloat16).astype(np.float64), axis, -1)
    blocks = v.reshape(v.shape[:-1] + (-1, 32))
    amax = np.abs(blocks).max(-1, keepdims=True)
    byte = np.maximum(np.where(amax > 0, np.frexp(amax)[1] - 1 + 127, 0) - down, 1)
    scale = np.exp2(byte - 127.0)
    codes = (blocks / scale).astype(np.float32).astype(dtype).astype(np.float64)
    return np.moveaxis((codes * scale).reshape(v.shape), -1, axis)


WIDE = False


def mx_kscale(k):
    if not WIDE:
        return np.ones(k)
    levels = np.array([10, -10, 5, -5, 0])
    if k % 512:
        return np.exp2(np.random.permutation(np.resize(levels, k // 32))).repeat(32)
    a = np.empty((k // 512, 16))
    for p in range(k // 512):
        a[p, :8] = np.random.permutation(np.resize(levels, 8))
        for g in range(8):
            far = levels[np.abs(levels - a[p, g]) >= 10]
            a[p, g + 8] = far[np.random.randint(len(far))]
    return np.exp2(a.ravel()).repeat(32)


def f64(x):
    return np.asarray(x).astype(np.float64)


def striped(idx):
    return np.tile(idx.reshape(-1, 16).T, (8, 1)).astype(np.uint16)


def unstriped(offs):
    return offs[:16].T.reshape(-1).astype(np.int64)


E2M1 = np.array([0.0, 0.5, 1.0, 1.5, 2.0, 3.0, 4.0, 6.0, -0.0, -0.5, -1.0, -1.5, -2.0, -3.0, -4.0, -6.0])


def pack_weight(w, fmt):
    k, n = w.shape
    w = f64(np.asarray(w, np.float32).astype(ml_dtypes.bfloat16)).reshape(k // 32, 32, n)
    amax = np.abs(w).max(1)
    if fmt == "e4m3":
        byte = np.frexp(amax)[1] - 1 + 127 - 7
    else:
        mant, ex = np.frexp(amax / 6.0)
        byte = np.where(mant > 0.5, ex, ex - 1) + 127
    byte = np.clip(np.where(amax > 0, byte, 1), 1, 254)
    scaled = (w * np.exp2(127.0 - byte)[:, None, :]).reshape(k, n).astype(np.float32)
    by_word = np.ascontiguousarray(scaled.reshape(k // 512, 128, 4, n).transpose(0, 1, 3, 2))
    if fmt == "e4m3":
        words = by_word.astype(ml_dtypes.float8_e4m3fn).view(np.uint8)
    else:
        c = by_word.astype(ml_dtypes.float4_e2m1fn).view(np.uint8) & 0xF
        words = (c[..., 0::2] | (c[..., 1::2] << 4)).reshape(k // 512, 128, 2 * n)
    return np.ascontiguousarray(words), np.ascontiguousarray(byte.astype(np.uint8).reshape(k // 512, 16, n))


def unpack_weight(words, scales, fmt):
    g, _, n = scales.shape
    words = np.ascontiguousarray(words).reshape(g, 128, n, -1)
    if fmt == "e4m3":
        vals = words.view(ml_dtypes.float8_e4m3fn).astype(np.float64)
    else:
        nib = np.empty((g, 128, n, 4), np.uint8)
        nib[..., 0::2] = words & 0xF
        nib[..., 1::2] = words >> 4
        vals = E2M1[nib]
    vals = vals * np.repeat(np.exp2(scales.astype(np.float64) - 127.0), 8, axis=1)[..., None]
    return vals.transpose(0, 1, 3, 2).reshape(g * 512, n)


def gelu(v):
    return 0.5 * v * (1.0 + np.tanh(np.sqrt(2.0 / np.pi) * (v + 0.044715 * v**3)))


K, T, H, S, T2, P, N = 1024, 4096, 512, 1024, 2048, 1024, 768


def setup_inputs():
    n = np.random.standard_normal
    s = mx_kscale(K)[:, None]
    u = mx_kscale(H)[:, None]
    tab_words, tab_scales = pack_weight(n((K, T)) * s, "e4m3")
    w2_words, w2_scales = pack_weight(1.2 * n((H, N)) / np.sqrt(H) / u, "e2m1")
    return {
        "tab_words": tab_words, "tab_scales": tab_scales,
        "offs": striped(np.random.permutation(T)[:S]),
        "offs2": striped(np.random.permutation(T2)[:S]),
        "offs3": striped(np.random.permutation(T2)[:P]),
        "w1": (n((K, H)) / np.sqrt(K) / s * u.T).astype(np.float32),
        "b1": (0.6 * n(H) * u[:, 0]).astype(np.float32),
        "salt": n((H, S)).astype(np.float32),
        "page0": (0.8 * n((H, T2)) * u).astype(np.float32),
        "w2_words": w2_words, "w2_scales": w2_scales,
        "w3": (0.52 * n((K, N)) / np.sqrt(K) / s).astype(np.float32),
        "notes": (0.5 * n((N, P))).astype(np.float32),
    }


def reference(tab_words, tab_scales, offs, offs2, offs3, w1, b1, salt, page0,
              w2_words, w2_scales, w3, notes):
    v = unpack_weight(tab_words, tab_scales, "e4m3")[:, unstriped(offs)]
    h = mxq(f64(w1), 0, "e4m3").T @ v
    h = (h + f64(b1)[:, None]) * f64(salt)
    page = f64(page0).copy()
    l2 = unstriped(offs2)
    page[:, l2] = page[:, l2] + h
    x = mxq(page[:, unstriped(offs3)], 0, "e4m3")
    y = unpack_weight(w2_words, w2_scales, "e2m1").T @ x
    ph = mxq(f64(w3), 0, "e4m3").T @ v
    return np.tanh(y) * np.cos(ph) + f64(notes)

@@ -1,0 +1,302 @@
+import math
+from contextlib import ExitStack
+
+import concourse.mybir as mybir
+from concourse.masks import make_identity
+
+K, T, H, S, T2, N = 1024, 4096, 512, 1024, 2048, 768
+FLOPS = 2 * K * H * S + 2 * H * N * S + 2 * K * N * S
+
+F32 = mybir.dt.float32
+BF16 = mybir.dt.bfloat16
+I32 = mybir.dt.int32
+U32 = mybir.dt.uint32
+U16 = mybir.dt.uint16
+U8 = mybir.dt.uint8
+FP8X4 = mybir.dt.float8_e4m3fn_x4
+FP4X4 = mybir.dt.float4_e2m1fn_x4
+ACT = mybir.ActivationFunctionType
+ALU = mybir.AluOpType
+
+P = 128
+PACK = 4
+PASSES = K // (P * PACK)
+BANK = 512
+CHUNK = 256
+CHUNKS = S // CHUNK
+NB = N // P
+ROUNDER = 1.5 * 2.0**23
+
+
+def tile_list_mast_corrosion_update_kernel(
+    tc, tab_words, tab_scales, offs, offs2, offs3, w1, b1, salt, page0, w2_words, w2_scales, w3, notes, out
+):
+    nc = tc.nc
+    with ExitStack() as ctx:
+        lists = ctx.enter_context(tc.tile_pool(name="lists", bufs=1))
+        sb = ctx.enter_context(tc.tile_pool(name="sb", bufs=1))
+        ps = ctx.enter_context(tc.psum_pool(name="ps", bufs=1))
+
+        def bank(tag, bufs):
+            return ps.tile([P, BANK], F32, name=tag, tag=tag, bufs=bufs)
+
+        idx1 = lists.tile([P, S // 16], U16, name="idx1")
+        idx2 = lists.tile([P, S // 16], U16, name="idx2")
+        idx3 = lists.tile([P, S // 16], U16, name="idx3")
+
+        page_rows = page0.rearrange("(p t) c -> p t c", t=PACK)
+        salt_rows = salt.rearrange("(p t) c -> p t c", t=PACK)
+        notes_rows = notes.rearrange("(b p) j -> p b j", p=P)
+        out_rows = out.rearrange("(b p) j -> p b j", p=P)
+
+        page = [sb.tile([P, T2], F32, name="page%d" % t) for t in range(PACK)]
+        salt_sb = [sb.tile([P, S], F32, name="salt%d" % t) for t in range(PACK)]
+        tab = [sb.tile([P, T], U32, name="tab%d" % a, tag="tab%d" % a, align_bytes=64) for a in range(PASSES)]
+        tab_sc = sb.tile([P, T], U8, name="tab_sc", align_bytes=64)
+        w1_raw = [sb.tile([P, PACK, H], F32, name="w1raw%d" % a, tag="w1raw%d" % a) for a in range(PASSES)]
+        w3_raw = [sb.tile([P, PACK, N], F32, name="w3raw%d" % a, tag="w3raw%d" % a) for a in range(PASSES)]
+        b1_sb = sb.tile([P, PACK], F32, name="b1_sb")
+        w2_sb = sb.tile([P, 2 * N], U8, name="w2_sb", align_bytes=64)
+        w2_sc = sb.tile([P, N], U8, name="w2_sc", align_bytes=64)
+        ident = sb.tile([P, P], F32, name="ident")
+
+        nc.vector.memset(tab_sc[:].bitcast(I32), 0)
+        nc.gpsimd.memset(w2_sc[:].bitcast(I32), 0)
+        make_identity(nc, ident[:])
+
+        nc.sync.dma_start(idx2[:], offs2)
+        nc.sync.dma_start(page[0][:], page_rows[:, 0, :])
+        nc.sync.dma_start(idx1[:], offs)
+        for q in range(4):
+            nc.scalar.dma_start(
+                tab_sc[32 * q : 32 * q + 4 * PASSES, :].bitcast(I32),
+                tab_scales[:, 4 * q : 4 * q + 4, :].bitcast(I32),
+            )
+        for a in range(PASSES):
+            nc.sync.dma_start(tab[a][:].bitcast(I32), tab_words[a].rearrange("p t i -> p (t i)").bitcast(I32))
+        for a in range(PASSES):
+            nc.sync.dma_start(w1_raw[a][:], w1[512 * a : 512 * (a + 1), :].rearrange("(p j) c -> p j c", j=PACK))
+        nc.sync.dma_start(b1_sb[:], b1.rearrange("(p t) -> p t", t=PACK))
+        nc.sync.dma_start(salt_sb[0][:], salt_rows[:, 0, :])
+        nc.sync.dma_start(idx3[:], offs3)
+        for a in range(PASSES):
+            nc.sync.dma_start(w3_raw[a][:], w3[512 * a : 512 * (a + 1), :].rearrange("(p j) c -> p j c", j=PACK))
+        for t in range(1, PACK):
+            nc.sync.dma_start(page[t][:], page_rows[:, t, :])
+            nc.sync.dma_start(salt_sb[t][:], salt_rows[:, t, :])
+        nc.sync.dma_start(w2_sb[:].bitcast(I32), w2_words[0].bitcast(I32))
+        for q in range(4):
+            nc.sync.dma_start(
+                w2_sc[32 * q : 32 * q + 4, :].bitcast(I32), w2_scales[0, 4 * q : 4 * q + 4, :].bitcast(I32)
+            )
+
+        old = [None] * PACK
+
+        def fetch_old(t):
+            old[t] = sb.tile([P, S], F32, name="old", tag="old", bufs=2)
+            nc.vector.tensor_copy(old[t][:], page[t][:].indirect(idx2[:]))
+
+        fetch_old(0)
+        v_sc = sb.tile([P, S], U8, name="v_sc", align_bytes=64)
+        nc.vector.tensor_copy(v_sc[:], tab_sc[:].indirect(idx1[:]))
+        v = [sb.tile([P, S], U32, name="v%d" % a, align_bytes=64) for a in range(PASSES)]
+        for a in range(PASSES):
+            nc.vector.tensor_copy(v[a][:], tab[a][:].indirect(idx1[:]))
+
+        notes_sb = [sb.tile([P, 2, NB, CHUNK], F32, name="notes%d" % a, tag="tab%d" % a, align_bytes=64) for a in range(2)]
+        for c in range(CHUNKS):
+            nc.sync.dma_start(notes_sb[c // 2][:, c % 2], notes_rows[:, :, c * CHUNK : (c + 1) * CHUNK])
+
+        w1_bf = sb.tile([P, PASSES, PACK, P, PACK], BF16, name="w1_bf", tag="w1_bf", align_bytes=64)
+        w1_q = [sb.tile([P, H], U32, name="w1q%d" % a, align_bytes=64) for a in range(PASSES)]
+        w1_s = [sb.tile([P, H], U8, name="w1s%d" % a, align_bytes=64) for a in range(PASSES)]
+
+        def w1_cast(engine_copy, a, t0, t1):
+            engine_copy(
+                w1_bf[:, a, t0:t1].rearrange("p t m j -> p m j t"),
+                w1_raw[a][:].rearrange("p j (m t) -> p m j t", t=PACK)[:, :, :, t0:t1],
+            )
+
+        def w1_quant(a, t0, t1):
+            nc.vector.quantize_mx(
+                out=w1_q[a][:, t0 * P : t1 * P].bitcast(FP8X4),
+                scales=w1_s[a][:, t0 * P : t1 * P],
+                in_=w1_bf[:, a, t0:t1].rearrange("p t m j -> p (t m j)"),
+            )
+
+        w1_cast(nc.vector.tensor_copy, 0, 0, 4)
+        w1_quant(0, 0, 4)
+        w1_cast(nc.vector.tensor_copy, 1, 0, 1)
+        w1_cast(nc.scalar.copy, 1, 1, 4)
+        w1_quant(1, 0, 1)
+
+        def h_matmul(t, half):
+            acc = bank("h", 2)
+            cols = slice(half * BANK, (half + 1) * BANK)
+            for a in range(PASSES):
+                nc.tensor.matmul_mx(
+                    out=acc[:],
+                    lhsT=w1_q[a][:, t * P : (t + 1) * P].bitcast(FP8X4),
+                    lhsT_scale=w1_s[a][:, t * P : (t + 1) * P],
+                    rhs=v[a][:, cols].bitcast(FP8X4),
+                    rhs_scale=v_sc[4 * a :, cols],
+                    start=(a == 0),
+                    stop=(a == PASSES - 1),
+                )
+            return acc
+
+        for half in range(2):
+            cols = slice(half * BANK, (half + 1) * BANK)
+            acc = h_matmul(0, half)
+            nc.vector.scalar_tensor_tensor(
+                out=salt_sb[0][:, cols], in0=acc[:], scalar=b1_sb[:, 0:1], in1=salt_sb[0][:, cols], op0=ALU.add, op1=ALU.mult
+            )
+        w1_quant(1, 1, 4)
+        for half in range(2):
+            cols = slice(half * BANK, (half + 1) * BANK)
+            nc.vector.tensor_tensor(
+                page[0][:].indirect(idx2[:, half * 32 : (half + 1) * 32]), old[0][:, cols], salt_sb[0][:, cols], ALU.add
+            )
+
+        hb_a = sb.tile([P, 2, S], F32, name="hb_a", tag="w1raw0")
+        hb_b = sb.tile([P, S], F32, name="hb_b", tag="w1raw1")
+        hb = [None, hb_a[:, 0, :], hb_a[:, 1, :], hb_b[:]]
+        for t in range(1, PACK):
+            for half in range(2):
+                cols = slice(half * BANK, (half + 1) * BANK)
+                acc = h_matmul(t, half)
+                nc.scalar.activation(hb[t][:, cols], acc[:], ACT.Identity, bias=b1_sb[:, t : t + 1])
+
+        x_bf = sb.tile([P, PACK, S], BF16, name="x_bf", tag="w1_bf", align_bytes=64)
+        nc.vector.tensor_copy(x_bf[:, 0, :], page[0][:].indirect(idx3[:]))
+
+        w3_q = [sb.tile([P, N], U32, name="w3q%d" % a, align_bytes=64) for a in range(PASSES)]
+        w3_s = [sb.tile([P, N], U8, name="w3s%d" % a, align_bytes=64) for a in range(PASSES)]
+        for a in range(PASSES):
+            w3_bf = sb.tile([P, N, PACK], BF16, name="w3bf%d" % a, tag="w3bf%d" % a, align_bytes=64)
+            for c0, c1 in ((0, 512), (512, N)):
+                nc.scalar.copy(
+                    w3_bf[:, c0:c1, :].rearrange("p (c i) j -> p c j i", i=4),
+                    w3_raw[a][:, :, c0:c1].rearrange("p j (c i) -> p c j i", i=4),
+                )
+                nc.vector.quantize_mx(
+                    out=w3_q[a][:, c0:c1].bitcast(FP8X4),
+                    scales=w3_s[a][:, c0:c1],
+                    in_=w3_bf[:, c0:c1, :].rearrange("p c j -> p (c j)"),
+                )
+
+        def update(t):
+            fetch_old(t)
+            nc.vector.tensor_tensor(salt_sb[t][:], hb[t], salt_sb[t][:], ALU.mult)
+            nc.vector.tensor_tensor(page[t][:].indirect(idx2[:]), old[t][:], salt_sb[t][:], ALU.add)
+
+        for t in range(1, PACK - 1):
+            update(t)
+            nc.vector.tensor_copy(x_bf[:, t, :], page[t][:].indirect(idx3[:]))
+        update(PACK - 1)
+
+        cos_sb = [sb.tile([P, 2, NB * CHUNK], F32, name="cos%d" % a, tag="w3raw%d" % a) for a in range(2)]
+        turns = [None] * CHUNKS
+        whole = [None] * CHUNKS
+
+        def phase(c):
+            turns[c] = sb.tile([P, 3 * BANK], F32, name="turns", tag="turns", bufs=2)
+            for i in range(3):
+                acc = bank("ph", 3)
+                if i < 2:
+                    parts = [(i, 0, 512, 0)]
+                else:
+                    parts = [(0, 512, N, 0), (1, 512, N, 256)]
+                for jl, n0, n1, o in parts:
+                    js = slice(c * CHUNK + jl * P, c * CHUNK + (jl + 1) * P)
+                    for a in range(PASSES):
+                        nc.tensor.matmul_mx(
+                            out=acc[:, o : o + n1 - n0],
+                            lhsT=v[a][:, js].bitcast(FP8X4),
+                            lhsT_scale=v_sc[4 * a :, js],
+                            rhs=w3_q[a][:, n0:n1].bitcast(FP8X4),
+                            rhs_scale=w3_s[a][:, n0:n1],
+                            start=(a == 0),
+                            stop=(a == PASSES - 1),
+                        )
+                nc.scalar.activation(
+                    turns[c][:, i * BANK : (i + 1) * BANK], acc[:], ACT.Copy, scale=1.0 / (2.0 * math.pi), bias=0.25
+                )
+            shifted = sb.tile([P, 3 * BANK], U32, name="shifted", tag="shifted", align_bytes=64)
+            nc.scalar.activation(shifted[:], turns[c][:], ACT.Copy, bias=ROUNDER)
+            whole[c] = sb.tile([P, 3 * BANK], F32, name="whole", tag="whole", bufs=2)
+            nc.scalar.activation(whole[c][:], shifted[:], ACT.Copy, scale=-1.0, bias=ROUNDER)
+
+        def cosine(c):
+            for i in range(3):
+                frac = bank("fr", 3)
+                for nl in range(2):
+                    nb = 2 * i + nl
+                    for jl in range(2):
+                        o = jl * 512 + nb * P if nb < 4 else 1024 + jl * 256 + (nb - 4) * P
+                        dst = frac[:, nl * CHUNK + jl * P : nl * CHUNK + (jl + 1) * P]
+                        nc.tensor.matmul(dst, turns[c][:, o : o + P], ident[:], is_transpose=True, start=True, stop=False)
+                        nc.tensor.matmul(dst, whole[c][:, o : o + P], ident[:], is_transpose=True, start=False, stop=True)
+                nc.scalar.activation(
+                    cos_sb[c // 2][:, c % 2, i * BANK : (i + 1) * BANK], frac[:], ACT.Sin, scale=2.0 * math.pi
+                )
+
+        phase(0)
+        for c in range(1, CHUNKS):
+            phase(c)
+            cosine(c - 1)
+        cosine(CHUNKS - 1)
+
+        x_il = sb.tile([P, S, PACK], BF16, name="x_il", tag="shifted", align_bytes=64)
+        x_q = sb.tile([P, S], U32, name="x_q", align_bytes=64)
+        x_s = sb.tile([P, S], U8, name="x_s", align_bytes=64)
+        for c in range(CHUNKS):
+            nc.vector.tensor_copy(
+                x_bf[:, PACK - 1, c * CHUNK : (c + 1) * CHUNK], page[PACK - 1][:].indirect(idx3[:, c * 16 : (c + 1) * 16])
+            )
+
+        def x_quant(c):
+            js = slice(c * CHUNK, (c + 1) * CHUNK)
+            nc.scalar.copy(
+                x_il[:, js, :].rearrange("p (c i) t -> p c t i", i=4),
+                x_bf[:, :, js].rearrange("p t (c i) -> p c t i", i=4),
+            )
+            nc.vector.quantize_mx(
+                out=x_q[:, js].bitcast(FP8X4), scales=x_s[:, js], in_=x_il[:, js, :].rearrange("p c t -> p (c t)")
+            )
+
+        pending = []
+
+        def finish():
+            c, i, th = pending.pop(0)
+            res = notes_sb[c // 2][:, c % 2, 2 * i : 2 * i + 2, :]
+            flat = res.rearrange("p b j -> p (b j)")
+            nc.vector.tensor_tensor(flat, th, flat, ALU.add)
+            nc.sync.dma_start(out_rows[:, 2 * i : 2 * i + 2, c * CHUNK : (c + 1) * CHUNK], res)
+
+        x_quant(0)
+        for c in range(CHUNKS):
+            js = slice(c * CHUNK, (c + 1) * CHUNK)
+            tanh_sb = sb.tile([P, 3 * BANK], F32, name="tanh_sb", tag="turns", bufs=2)
+            for i in range(3):
+                acc = bank("fr", 3) if c % 2 == 0 else bank("ph", 3)
+                for nl in range(2):
+                    nb = 2 * i + nl
+                    nc.tensor.matmul_mx(
+                        out=acc[:, nl * CHUNK : (nl + 1) * CHUNK],
+                        lhsT=w2_sb[:, 2 * nb * P : 2 * (nb + 1) * P].bitcast(FP4X4),
+                        lhsT_scale=w2_sc[:, nb * P : (nb + 1) * P],
+                        rhs=x_q[:, js].bitcast(FP8X4),
+                        rhs_scale=x_s[:, js],
+                        start=True,
+                        stop=True,
+                    )
+                th = tanh_sb[:, i * BANK : (i + 1) * BANK]
+                nc.scalar.activation(th, acc[:], ACT.Tanh)
+                if i == 0 and c + 1 < CHUNKS:
+                    x_quant(c + 1)
+                nc.vector.tensor_tensor(th, th, cos_sb[c // 2][:, c % 2, i * BANK : (i + 1) * BANK], ALU.mult)
+                if pending:
+                    finish()
+                pending.append((c, i, th))
+        finish()

@@ -52,7 +52,7 @@ def tile_list_mast_corrosion_update_kernel(
         page = [sb.tile([P, T2], F32, name="page%d" % t) for t in range(PACK)]
         salt_sb = [sb.tile([P, S], F32, name="salt%d" % t) for t in range(PACK)]
         tab = [sb.tile([P, T], U32, name="tab%d" % a, tag="tab%d" % a, align_bytes=64) for a in range(PASSES)]
-        tab_sc = sb.tile([P, T], U8, name="tab_sc", align_bytes=64)
+        tab_sc = sb.tile([P, T], U8, name="tab_sc", tag="tab_sc", align_bytes=64)
         w1_raw = [sb.tile([P, PACK, H], F32, name="w1raw%d" % a, tag="w1raw%d" % a) for a in range(PASSES)]
         w3_raw = [sb.tile([P, PACK, N], F32, name="w3raw%d" % a, tag="w3raw%d" % a) for a in range(PASSES)]
         b1_sb = sb.tile([P, PACK], F32, name="b1_sb")
@@ -61,17 +61,21 @@ def tile_list_mast_corrosion_update_kernel(
         ident = sb.tile([P, P], F32, name="ident")
 
         nc.vector.memset(tab_sc[:].bitcast(I32), 0)
-        nc.gpsimd.memset(w2_sc[:].bitcast(I32), 0)
+        nc.vector.memset(w2_sc[:].bitcast(I32), 0)
+        for q in range(4):
+            nc.gpsimd.dma_start(
+                tab_sc[32 * q : 32 * q + 4 * PASSES, :].bitcast(I32),
+                tab_scales[:, 4 * q : 4 * q + 4, :].bitcast(I32),
+            )
+        for q in range(4):
+            nc.gpsimd.dma_start(
+                w2_sc[32 * q : 32 * q + 4, :].bitcast(I32), w2_scales[0, 4 * q : 4 * q + 4, :].bitcast(I32)
+            )
         make_identity(nc, ident[:])
 
         nc.sync.dma_start(idx2[:], offs2)
         nc.sync.dma_start(page[0][:], page_rows[:, 0, :])
         nc.sync.dma_start(idx1[:], offs)
-        for q in range(4):
-            nc.scalar.dma_start(
-                tab_sc[32 * q : 32 * q + 4 * PASSES, :].bitcast(I32),
-                tab_scales[:, 4 * q : 4 * q + 4, :].bitcast(I32),
-            )
         for a in range(PASSES):
             nc.sync.dma_start(tab[a][:].bitcast(I32), tab_words[a].rearrange("p t i -> p (t i)").bitcast(I32))
         for a in range(PASSES):
@@ -85,10 +89,6 @@ def tile_list_mast_corrosion_update_kernel(
             nc.sync.dma_start(page[t][:], page_rows[:, t, :])
             nc.sync.dma_start(salt_sb[t][:], salt_rows[:, t, :])
         nc.sync.dma_start(w2_sb[:].bitcast(I32), w2_words[0].bitcast(I32))
-        for q in range(4):
-            nc.sync.dma_start(
-                w2_sc[32 * q : 32 * q + 4, :].bitcast(I32), w2_scales[0, 4 * q : 4 * q + 4, :].bitcast(I32)
-            )
 
         old = [None] * PACK
 
@@ -107,28 +107,29 @@ def tile_list_mast_corrosion_update_kernel(
         for c in range(CHUNKS):
             nc.sync.dma_start(notes_sb[c // 2][:, c % 2], notes_rows[:, :, c * CHUNK : (c + 1) * CHUNK])
 
-        w1_bf = sb.tile([P, PASSES, PACK, P, PACK], BF16, name="w1_bf", tag="w1_bf", align_bytes=64)
+        w1_bf = {}
         w1_q = [sb.tile([P, H], U32, name="w1q%d" % a, align_bytes=64) for a in range(PASSES)]
         w1_s = [sb.tile([P, H], U8, name="w1s%d" % a, align_bytes=64) for a in range(PASSES)]
 
         def w1_cast(engine_copy, a, t0, t1):
+            w1_bf[a, t0] = sb.tile([P, t1 - t0, P, PACK], BF16, name="w1bf%d%d" % (a, t0), align_bytes=64)
             engine_copy(
-                w1_bf[:, a, t0:t1].rearrange("p t m j -> p m j t"),
-                w1_raw[a][:].rearrange("p j (m t) -> p m j t", t=PACK)[:, :, :, t0:t1],
+                w1_bf[a, t0][:].rearrange("p t m j -> p m t j"),
+                w1_raw[a][:].rearrange("p j (m t) -> p m t j", t=PACK)[:, :, t0:t1, :],
             )
 
         def w1_quant(a, t0, t1):
             nc.vector.quantize_mx(
                 out=w1_q[a][:, t0 * P : t1 * P].bitcast(FP8X4),
                 scales=w1_s[a][:, t0 * P : t1 * P],
-                in_=w1_bf[:, a, t0:t1].rearrange("p t m j -> p (t m j)"),
+                in_=w1_bf[a, t0][:].rearrange("p t m j -> p (t m j)"),
             )
 
-        w1_cast(nc.vector.tensor_copy, 0, 0, 4)
-        w1_quant(0, 0, 4)
-        w1_cast(nc.vector.tensor_copy, 1, 0, 1)
-        w1_cast(nc.scalar.copy, 1, 1, 4)
-        w1_quant(1, 0, 1)
+        for a in range(PASSES):
+            w1_cast(nc.vector.tensor_copy, a, 0, 1)
+            w1_cast(nc.scalar.copy, a, 1, PACK)
+            w1_quant(a, 0, 1)
+        w1_quant(0, 1, PACK)
 
         def h_matmul(t, half):
             acc = bank("h", 2)
@@ -159,15 +160,18 @@ def tile_list_mast_corrosion_update_kernel(
             )
 
         hb_a = sb.tile([P, 2, S], F32, name="hb_a", tag="w1raw0")
-        hb_b = sb.tile([P, S], F32, name="hb_b", tag="w1raw1")
+        hb_b = sb.tile([P, S], F32, name="hb_b", tag="tab_sc", align_bytes=64)
         hb = [None, hb_a[:, 0, :], hb_a[:, 1, :], hb_b[:]]
-        for t in range(1, PACK):
+
+        def features(t):
             for half in range(2):
                 cols = slice(half * BANK, (half + 1) * BANK)
                 acc = h_matmul(t, half)
                 nc.scalar.activation(hb[t][:, cols], acc[:], ACT.Identity, bias=b1_sb[:, t : t + 1])
 
-        x_bf = sb.tile([P, PACK, S], BF16, name="x_bf", tag="w1_bf", align_bytes=64)
+        features(1)
+
+        x_bf = sb.tile([P, PACK, S], BF16, name="x_bf", tag="w1raw1")
         nc.vector.tensor_copy(x_bf[:, 0, :], page[0][:].indirect(idx3[:]))
 
         w3_q = [sb.tile([P, N], U32, name="w3q%d" % a, align_bytes=64) for a in range(PASSES)]
@@ -185,10 +189,16 @@ def tile_list_mast_corrosion_update_kernel(
                     in_=w3_bf[:, c0:c1, :].rearrange("p c j -> p (c j)"),
                 )
 
+        for t in range(2, PACK):
+            features(t)
+
         def update(t):
             fetch_old(t)
-            nc.vector.tensor_tensor(salt_sb[t][:], hb[t], salt_sb[t][:], ALU.mult)
-            nc.vector.tensor_tensor(page[t][:].indirect(idx2[:]), old[t][:], salt_sb[t][:], ALU.add)
+            salted = salt_sb[t]
+            if t == 1:
+                salted = sb.tile([P, S], F32, name="salted", tag="w3bf1", align_bytes=64)
+            nc.vector.tensor_tensor(salted[:], hb[t], salt_sb[t][:], ALU.mult)
+            nc.vector.tensor_tensor(page[t][:].indirect(idx2[:]), old[t][:], salted[:], ALU.add)
 
         for t in range(1, PACK - 1):
             update(t)
@@ -200,7 +210,7 @@ def tile_list_mast_corrosion_update_kernel(
         whole = [None] * CHUNKS
 
         def phase(c):
-            turns[c] = sb.tile([P, 3 * BANK], F32, name="turns", tag="turns", bufs=2)
+            turns[c] = sb.tile([P, 3 * BANK], F32, name="turns", tag="turns", bufs=CHUNKS)
             for i in range(3):
                 acc = bank("ph", 3)
                 if i < 2:
@@ -222,9 +232,14 @@ def tile_list_mast_corrosion_update_kernel(
                 nc.scalar.activation(
                     turns[c][:, i * BANK : (i + 1) * BANK], acc[:], ACT.Copy, scale=1.0 / (2.0 * math.pi), bias=0.25
                 )
+
+        def nearest(c):
             shifted = sb.tile([P, 3 * BANK], U32, name="shifted", tag="shifted", align_bytes=64)
             nc.scalar.activation(shifted[:], turns[c][:], ACT.Copy, bias=ROUNDER)
-            whole[c] = sb.tile([P, 3 * BANK], F32, name="whole", tag="whole", bufs=2)
+            if c + 1 < CHUNKS:
+                whole[c] = sb.tile([P, 3 * BANK], F32, name="whole", tag="whole", bufs=2)
+            else:
+                whole[c] = sb.tile([P, 3 * BANK], F32, name="whole_last", tag="whole_last", align_bytes=64)
             nc.scalar.activation(whole[c][:], shifted[:], ACT.Copy, scale=-1.0, bias=ROUNDER)
 
         def cosine(c):
@@ -241,13 +256,15 @@ def tile_list_mast_corrosion_update_kernel(
                     cos_sb[c // 2][:, c % 2, i * BANK : (i + 1) * BANK], frac[:], ACT.Sin, scale=2.0 * math.pi
                 )
 
-        phase(0)
-        for c in range(1, CHUNKS):
+        for c in range(CHUNKS):
             phase(c)
+        nearest(0)
+        for c in range(1, CHUNKS):
+            nearest(c)
             cosine(c - 1)
         cosine(CHUNKS - 1)
 
-        x_il = sb.tile([P, S, PACK], BF16, name="x_il", tag="shifted", align_bytes=64)
+        x_il = sb.tile([P, S, PACK], BF16, name="x_il", tag="whole_last", align_bytes=64)
         x_q = sb.tile([P, S], U32, name="x_q", align_bytes=64)
         x_s = sb.tile([P, S], U8, name="x_s", align_bytes=64)
         for c in range(CHUNKS):
@@ -277,7 +294,7 @@ def tile_list_mast_corrosion_update_kernel(
         x_quant(0)
         for c in range(CHUNKS):
             js = slice(c * CHUNK, (c + 1) * CHUNK)
-            tanh_sb = sb.tile([P, 3 * BANK], F32, name="tanh_sb", tag="turns", bufs=2)
+            tanh_sb = sb.tile([P, 3 * BANK], F32, name="tanh_sb", tag="turns", bufs=CHUNKS)
             for i in range(3):
                 acc = bank("fr", 3) if c % 2 == 0 else bank("ph", 3)
                 for nl in range(2):

@@ -87,13 +87,14 @@ def tile_list_mast_corrosion_update_kernel(
             nc.sync.dma_start(w3_raw[a][:], w3[512 * a : 512 * (a + 1), :].rearrange("(p j) c -> p j c", j=PACK))
         for t in range(1, PACK):
             nc.sync.dma_start(page[t][:], page_rows[:, t, :])
+        for t in range(1, PACK):
             nc.sync.dma_start(salt_sb[t][:], salt_rows[:, t, :])
         nc.sync.dma_start(w2_sb[:].bitcast(I32), w2_words[0].bitcast(I32))
 
         old = [None] * PACK
 
         def fetch_old(t):
-            old[t] = sb.tile([P, S], F32, name="old", tag="old", bufs=2)
+            old[t] = sb.tile([P, S], F32, name="old%d" % t, tag="old%d" % t)
             nc.vector.tensor_copy(old[t][:], page[t][:].indirect(idx2[:]))
 
         fetch_old(0)
@@ -193,12 +194,13 @@ def tile_list_mast_corrosion_update_kernel(
             features(t)
 
         def update(t):
+            halves = [slice(half * BANK, (half + 1) * BANK) for half in range(2)]
+            for cols in halves:
+                nc.gpsimd.tensor_tensor(salt_sb[t][:, cols], hb[t][:, cols], salt_sb[t][:, cols], ALU.mult)
             fetch_old(t)
-            salted = salt_sb[t]
-            if t == 1:
-                salted = sb.tile([P, S], F32, name="salted", tag="w3bf1", align_bytes=64)
-            nc.vector.tensor_tensor(salted[:], hb[t], salt_sb[t][:], ALU.mult)
-            nc.vector.tensor_tensor(page[t][:].indirect(idx2[:]), old[t][:], salted[:], ALU.add)
+            for cols in halves:
+                nc.gpsimd.tensor_tensor(salt_sb[t][:, cols], old[t][:, cols], salt_sb[t][:, cols], ALU.add)
+            nc.vector.tensor_copy(page[t][:].indirect(idx2[:]), salt_sb[t][:])
 
         for t in range(1, PACK - 1):
             update(t)
@@ -234,13 +236,17 @@ def tile_list_mast_corrosion_update_kernel(
                 )
 
         def nearest(c):
-            shifted = sb.tile([P, 3 * BANK], U32, name="shifted", tag="shifted", align_bytes=64)
-            nc.scalar.activation(shifted[:], turns[c][:], ACT.Copy, bias=ROUNDER)
+            if c < CHUNKS // 2:
+                shifted = sb.tile([P, 3 * BANK], U32, name="shifted", tag="old%d" % c)
+                nc.scalar.activation(shifted[:], turns[c][:], ACT.Copy, bias=ROUNDER)
+            else:
+                shifted = sb.tile([P, 3 * BANK], I32, name="shifted", tag="old%d" % (PACK + 1 - c))
+                nc.gpsimd.tensor_scalar(shifted[:], turns[c][:], 1.0, ROUNDER, ALU.mult, ALU.add)
             if c + 1 < CHUNKS:
-                whole[c] = sb.tile([P, 3 * BANK], F32, name="whole", tag="whole", bufs=2)
+                whole[c] = sb.tile([P, 3 * BANK], F32, name="whole", tag="w3bf%d" % (c % 2), align_bytes=64)
             else:
                 whole[c] = sb.tile([P, 3 * BANK], F32, name="whole_last", tag="whole_last", align_bytes=64)
-            nc.scalar.activation(whole[c][:], shifted[:], ACT.Copy, scale=-1.0, bias=ROUNDER)
+            nc.scalar.activation(whole[c][:], shifted[:].bitcast(U32), ACT.Copy, scale=-1.0, bias=ROUNDER)
 
         def cosine(c):
             for i in range(3):

import math
from contextlib import ExitStack

import concourse.mybir as mybir
from concourse.masks import make_identity

K, T, H, S, T2, N = 1024, 4096, 512, 1024, 2048, 768
FLOPS = 2 * K * H * S + 2 * H * N * S + 2 * K * N * S

F32 = mybir.dt.float32
BF16 = mybir.dt.bfloat16
I32 = mybir.dt.int32
U32 = mybir.dt.uint32
U16 = mybir.dt.uint16
U8 = mybir.dt.uint8
FP8X4 = mybir.dt.float8_e4m3fn_x4
FP4X4 = mybir.dt.float4_e2m1fn_x4
ACT = mybir.ActivationFunctionType
ALU = mybir.AluOpType

P = 128
PACK = 4
PASSES = K // (P * PACK)
BANK = 512
CHUNK = 256
CHUNKS = S // CHUNK
NB = N // P
ROUNDER = 1.5 * 2.0**23


def tile_list_mast_corrosion_update_kernel(
    tc, tab_words, tab_scales, offs, offs2, offs3, w1, b1, salt, page0, w2_words, w2_scales, w3, notes, out
):
    nc = tc.nc
    with ExitStack() as ctx:
        lists = ctx.enter_context(tc.tile_pool(name="lists", bufs=1))
        sb = ctx.enter_context(tc.tile_pool(name="sb", bufs=1))
        ps = ctx.enter_context(tc.psum_pool(name="ps", bufs=1))

        def bank(tag, bufs):
            return ps.tile([P, BANK], F32, name=tag, tag=tag, bufs=bufs)

        idx1 = lists.tile([P, S // 16], U16, name="idx1")
        idx2 = lists.tile([P, S // 16], U16, name="idx2")
        idx3 = lists.tile([P, S // 16], U16, name="idx3")

        page_rows = page0.rearrange("(p t) c -> p t c", t=PACK)
        salt_rows = salt.rearrange("(p t) c -> p t c", t=PACK)
        notes_rows = notes.rearrange("(b p) j -> p b j", p=P)
        out_rows = out.rearrange("(b p) j -> p b j", p=P)

        page = [sb.tile([P, T2], F32, name="page%d" % t) for t in range(PACK)]
        salt_sb = [sb.tile([P, S], F32, name="salt%d" % t) for t in range(PACK)]
        tab = [sb.tile([P, T], U32, name="tab%d" % a, tag="tab%d" % a, align_bytes=64) for a in range(PASSES)]
        tab_sc = sb.tile([P, T], U8, name="tab_sc", tag="tab_sc", align_bytes=64)
        w1_raw = [sb.tile([P, PACK, H], F32, name="w1raw%d" % a, tag="w1raw%d" % a) for a in range(PASSES)]
        w3_raw = [sb.tile([P, PACK, N], F32, name="w3raw%d" % a, tag="w3raw%d" % a) for a in range(PASSES)]
        b1_sb = sb.tile([P, PACK], F32, name="b1_sb")
        w2_sb = sb.tile([P, 2 * N], U8, name="w2_sb", align_bytes=64)
        w2_sc = sb.tile([P, N], U8, name="w2_sc", align_bytes=64)
        ident = sb.tile([P, P], F32, name="ident")

        nc.vector.memset(tab_sc[:].bitcast(I32), 0)
        nc.vector.memset(w2_sc[:].bitcast(I32), 0)
        for q in range(4):
            nc.gpsimd.dma_start(
                tab_sc[32 * q : 32 * q + 4 * PASSES, :].bitcast(I32),
                tab_scales[:, 4 * q : 4 * q + 4, :].bitcast(I32),
            )
        for q in range(4):
            nc.gpsimd.dma_start(
                w2_sc[32 * q : 32 * q + 4, :].bitcast(I32), w2_scales[0, 4 * q : 4 * q + 4, :].bitcast(I32)
            )
        make_identity(nc, ident[:])

        nc.sync.dma_start(idx2[:], offs2)
        nc.sync.dma_start(page[0][:], page_rows[:, 0, :])
        nc.sync.dma_start(idx1[:], offs)
        for a in range(PASSES):
            nc.sync.dma_start(tab[a][:].bitcast(I32), tab_words[a].rearrange("p t i -> p (t i)").bitcast(I32))
        for a in range(PASSES):
            nc.sync.dma_start(w1_raw[a][:], w1[512 * a : 512 * (a + 1), :].rearrange("(p j) c -> p j c", j=PACK))
        nc.sync.dma_start(b1_sb[:], b1.rearrange("(p t) -> p t", t=PACK))
        nc.sync.dma_start(salt_sb[0][:], salt_rows[:, 0, :])
        nc.sync.dma_start(idx3[:], offs3)
        for a in range(PASSES):
            nc.sync.dma_start(w3_raw[a][:], w3[512 * a : 512 * (a + 1), :].rearrange("(p j) c -> p j c", j=PACK))
        for t in range(1, PACK):
            nc.sync.dma_start(page[t][:], page_rows[:, t, :])
        for t in range(1, PACK):
            nc.sync.dma_start(salt_sb[t][:], salt_rows[:, t, :])
        nc.sync.dma_start(w2_sb[:].bitcast(I32), w2_words[0].bitcast(I32))

        old = [None] * PACK

        def fetch_old(t):
            old[t] = sb.tile([P, S], F32, name="old%d" % t, tag="old%d" % t)
            nc.vector.tensor_copy(old[t][:], page[t][:].indirect(idx2[:]))

        fetch_old(0)
        v_sc = sb.tile([P, S], U8, name="v_sc", align_bytes=64)
        nc.vector.tensor_copy(v_sc[:], tab_sc[:].indirect(idx1[:]))
        v = [sb.tile([P, S], U32, name="v%d" % a, align_bytes=64) for a in range(PASSES)]
        for a in range(PASSES):
            nc.vector.tensor_copy(v[a][:], tab[a][:].indirect(idx1[:]))

        notes_sb = [sb.tile([P, 2, NB, CHUNK], F32, name="notes%d" % a, tag="tab%d" % a, align_bytes=64) for a in range(2)]
        for c in range(CHUNKS):
            nc.sync.dma_start(notes_sb[c // 2][:, c % 2], notes_rows[:, :, c * CHUNK : (c + 1) * CHUNK])

        w1_bf = {}
        w1_q = [sb.tile([P, H], U32, name="w1q%d" % a, align_bytes=64) for a in range(PASSES)]
        w1_s = [sb.tile([P, H], U8, name="w1s%d" % a, align_bytes=64) for a in range(PASSES)]

        def w1_cast(engine_copy, a, t0, t1):
            w1_bf[a, t0] = sb.tile([P, t1 - t0, P, PACK], BF16, name="w1bf%d%d" % (a, t0), align_bytes=64)
            engine_copy(
                w1_bf[a, t0][:].rearrange("p t m j -> p m t j"),
                w1_raw[a][:].rearrange("p j (m t) -> p m t j", t=PACK)[:, :, t0:t1, :],
            )

        def w1_quant(a, t0, t1):
            nc.vector.quantize_mx(
                out=w1_q[a][:, t0 * P : t1 * P].bitcast(FP8X4),
                scales=w1_s[a][:, t0 * P : t1 * P],
                in_=w1_bf[a, t0][:].rearrange("p t m j -> p (t m j)"),
            )

        for a in range(PASSES):
            w1_cast(nc.vector.tensor_copy, a, 0, 1)
            w1_cast(nc.scalar.copy, a, 1, PACK)
            w1_quant(a, 0, 1)
        w1_quant(0, 1, PACK)

        def h_matmul(t, half):
            acc = bank("h", 2)
            cols = slice(half * BANK, (half + 1) * BANK)
            for a in range(PASSES):
                nc.tensor.matmul_mx(
                    out=acc[:],
                    lhsT=w1_q[a][:, t * P : (t + 1) * P].bitcast(FP8X4),
                    lhsT_scale=w1_s[a][:, t * P : (t + 1) * P],
                    rhs=v[a][:, cols].bitcast(FP8X4),
                    rhs_scale=v_sc[4 * a :, cols],
                    start=(a == 0),
                    stop=(a == PASSES - 1),
                )
            return acc

        for half in range(2):
            cols = slice(half * BANK, (half + 1) * BANK)
            acc = h_matmul(0, half)
            nc.vector.scalar_tensor_tensor(
                out=salt_sb[0][:, cols], in0=acc[:], scalar=b1_sb[:, 0:1], in1=salt_sb[0][:, cols], op0=ALU.add, op1=ALU.mult
            )
        w1_quant(1, 1, 4)
        for half in range(2):
            cols = slice(half * BANK, (half + 1) * BANK)
            nc.vector.tensor_tensor(
                page[0][:].indirect(idx2[:, half * 32 : (half + 1) * 32]), old[0][:, cols], salt_sb[0][:, cols], ALU.add
            )

        hb_a = sb.tile([P, 2, S], F32, name="hb_a", tag="w1raw0")
        hb_b = sb.tile([P, S], F32, name="hb_b", tag="tab_sc", align_bytes=64)
        hb = [None, hb_a[:, 0, :], hb_a[:, 1, :], hb_b[:]]

        def features(t):
            for half in range(2):
                cols = slice(half * BANK, (half + 1) * BANK)
                acc = h_matmul(t, half)
                nc.scalar.activation(hb[t][:, cols], acc[:], ACT.Identity, bias=b1_sb[:, t : t + 1])

        features(1)

        x_bf = sb.tile([P, PACK, S], BF16, name="x_bf", tag="w1raw1")
        nc.vector.tensor_copy(x_bf[:, 0, :], page[0][:].indirect(idx3[:]))

        w3_q = [sb.tile([P, N], U32, name="w3q%d" % a, align_bytes=64) for a in range(PASSES)]
        w3_s = [sb.tile([P, N], U8, name="w3s%d" % a, align_bytes=64) for a in range(PASSES)]
        for a in range(PASSES):
            w3_bf = sb.tile([P, N, PACK], BF16, name="w3bf%d" % a, tag="w3bf%d" % a, align_bytes=64)
            for c0, c1 in ((0, 512), (512, N)):
                nc.scalar.copy(
                    w3_bf[:, c0:c1, :].rearrange("p (c i) j -> p c j i", i=4),
                    w3_raw[a][:, :, c0:c1].rearrange("p j (c i) -> p c j i", i=4),
                )
                nc.vector.quantize_mx(
                    out=w3_q[a][:, c0:c1].bitcast(FP8X4),
                    scales=w3_s[a][:, c0:c1],
                    in_=w3_bf[:, c0:c1, :].rearrange("p c j -> p (c j)"),
                )

        for t in range(2, PACK):
            features(t)

        def update(t):
            halves = [slice(half * BANK, (half + 1) * BANK) for half in range(2)]
            for cols in halves:
                nc.gpsimd.tensor_tensor(salt_sb[t][:, cols], hb[t][:, cols], salt_sb[t][:, cols], ALU.mult)
            fetch_old(t)
            for cols in halves:
                nc.gpsimd.tensor_tensor(salt_sb[t][:, cols], old[t][:, cols], salt_sb[t][:, cols], ALU.add)
            nc.vector.tensor_copy(page[t][:].indirect(idx2[:]), salt_sb[t][:])

        for t in range(1, PACK - 1):
            update(t)
            nc.vector.tensor_copy(x_bf[:, t, :], page[t][:].indirect(idx3[:]))
        update(PACK - 1)

        cos_sb = [sb.tile([P, 2, NB * CHUNK], F32, name="cos%d" % a, tag="w3raw%d" % a) for a in range(2)]
        turns = [None] * CHUNKS
        whole = [None] * CHUNKS

        def phase(c):
            turns[c] = sb.tile([P, 3 * BANK], F32, name="turns", tag="turns", bufs=CHUNKS)
            for i in range(3):
                acc = bank("ph", 3)
                if i < 2:
                    parts = [(i, 0, 512, 0)]
                else:
                    parts = [(0, 512, N, 0), (1, 512, N, 256)]
                for jl, n0, n1, o in parts:
                    js = slice(c * CHUNK + jl * P, c * CHUNK + (jl + 1) * P)
                    for a in range(PASSES):
                        nc.tensor.matmul_mx(
                            out=acc[:, o : o + n1 - n0],
                            lhsT=v[a][:, js].bitcast(FP8X4),
                            lhsT_scale=v_sc[4 * a :, js],
                            rhs=w3_q[a][:, n0:n1].bitcast(FP8X4),
                            rhs_scale=w3_s[a][:, n0:n1],
                            start=(a == 0),
                            stop=(a == PASSES - 1),
                        )
                nc.scalar.activation(
                    turns[c][:, i * BANK : (i + 1) * BANK], acc[:], ACT.Copy, scale=1.0 / (2.0 * math.pi), bias=0.25
                )

        def nearest(c):
            if c < CHUNKS // 2:
                shifted = sb.tile([P, 3 * BANK], U32, name="shifted", tag="old%d" % c)
                nc.scalar.activation(shifted[:], turns[c][:], ACT.Copy, bias=ROUNDER)
            else:
                shifted = sb.tile([P, 3 * BANK], I32, name="shifted", tag="old%d" % (PACK + 1 - c))
                nc.gpsimd.tensor_scalar(shifted[:], turns[c][:], 1.0, ROUNDER, ALU.mult, ALU.add)
            if c + 1 < CHUNKS:
                whole[c] = sb.tile([P, 3 * BANK], F32, name="whole", tag="w3bf%d" % (c % 2), align_bytes=64)
            else:
                whole[c] = sb.tile([P, 3 * BANK], F32, name="whole_last", tag="whole_last", align_bytes=64)
            nc.scalar.activation(whole[c][:], shifted[:].bitcast(U32), ACT.Copy, scale=-1.0, bias=ROUNDER)

        def cosine(c):
            for i in range(3):
                frac = bank("fr", 3)
                for nl in range(2):
                    nb = 2 * i + nl
                    for jl in range(2):
                        o = jl * 512 + nb * P if nb < 4 else 1024 + jl * 256 + (nb - 4) * P
                        dst = frac[:, nl * CHUNK + jl * P : nl * CHUNK + (jl + 1) * P]
                        nc.tensor.matmul(dst, turns[c][:, o : o + P], ident[:], is_transpose=True, start=True, stop=False)
                        nc.tensor.matmul(dst, whole[c][:, o : o + P], ident[:], is_transpose=True, start=False, stop=True)
                nc.scalar.activation(
                    cos_sb[c // 2][:, c % 2, i * BANK : (i + 1) * BANK], frac[:], ACT.Sin, scale=2.0 * math.pi
                )

        for c in range(CHUNKS):
            phase(c)
        nearest(0)
        for c in range(1, CHUNKS):
            nearest(c)
            cosine(c - 1)
        cosine(CHUNKS - 1)

        x_il = sb.tile([P, S, PACK], BF16, name="x_il", tag="whole_last", align_bytes=64)
        x_q = sb.tile([P, S], U32, name="x_q", align_bytes=64)
        x_s = sb.tile([P, S], U8, name="x_s", align_bytes=64)
        for c in range(CHUNKS):
            nc.vector.tensor_copy(
                x_bf[:, PACK - 1, c * CHUNK : (c + 1) * CHUNK], page[PACK - 1][:].indirect(idx3[:, c * 16 : (c + 1) * 16])
            )

        def x_quant(c):
            js = slice(c * CHUNK, (c + 1) * CHUNK)
            nc.scalar.copy(
                x_il[:, js, :].rearrange("p (c i) t -> p c t i", i=4),
                x_bf[:, :, js].rearrange("p t (c i) -> p c t i", i=4),
            )
            nc.vector.quantize_mx(
                out=x_q[:, js].bitcast(FP8X4), scales=x_s[:, js], in_=x_il[:, js, :].rearrange("p c t -> p (c t)")
            )

        pending = []

        def finish():
            c, i, th = pending.pop(0)
            res = notes_sb[c // 2][:, c % 2, 2 * i : 2 * i + 2, :]
            flat = res.rearrange("p b j -> p (b j)")
            nc.vector.tensor_tensor(flat, th, flat, ALU.add)
            nc.sync.dma_start(out_rows[:, 2 * i : 2 * i + 2, c * CHUNK : (c + 1) * CHUNK], res)

        x_quant(0)
        for c in range(CHUNKS):
            js = slice(c * CHUNK, (c + 1) * CHUNK)
            tanh_sb = sb.tile([P, 3 * BANK], F32, name="tanh_sb", tag="turns", bufs=CHUNKS)
            for i in range(3):
                acc = bank("fr", 3) if c % 2 == 0 else bank("ph", 3)
                for nl in range(2):
                    nb = 2 * i + nl
                    nc.tensor.matmul_mx(
                        out=acc[:, nl * CHUNK : (nl + 1) * CHUNK],
                        lhsT=w2_sb[:, 2 * nb * P : 2 * (nb + 1) * P].bitcast(FP4X4),
                        lhsT_scale=w2_sc[:, nb * P : (nb + 1) * P],
                        rhs=x_q[:, js].bitcast(FP8X4),
                        rhs_scale=x_s[:, js],
                        start=True,
                        stop=True,
                    )
                th = tanh_sb[:, i * BANK : (i + 1) * BANK]
                nc.scalar.activation(th, acc[:], ACT.Tanh)
                if i == 0 and c + 1 < CHUNKS:
                    x_quant(c + 1)
                nc.vector.tensor_tensor(th, th, cos_sb[c // 2][:, c % 2, i * BANK : (i + 1) * BANK], ALU.mult)
                if pending:
                    finish()
                pending.append((c, i, th))
        finish()
